import numpy as np
CORES = [2,5,10,13,18,21,26,29,34,37,42,45]
N = 12
def setup_inputs(rng):
    return {"x": rng.standard_normal((N, 128, 2), dtype=np.float32)}
def reference(x):
    s = x.sum(axis=0, dtype=np.float64).astype(x.dtype)
    return {"y": np.broadcast_to(s, (N,) + s.shape)}

@@ -1,0 +1,65 @@
+import concourse.bass as bass
+from concourse.mybir import AluOpType
+
+WHERE = "sbuf"
+HELPER = 3
+M_GATHER = 0x00FF
+M_ON = 0xFF00
+M_MATE = 0x00FF
+
+SCRATCH = {
+    "xs": (WHERE, [128, 2], "float32"),
+    "land": (WHERE, [128, 12], "float32"),
+    "a": (WHERE, [128, 2], "float32"),
+    "b": (WHERE, [128, 2], "float32"),
+}
+SEMAPHORES = ["local", "sent", "arr", "got_a", "got_b"]
+
+
+def bits(m):
+    return bin(m).count("1")
+
+
+def dst_id(topo, c):
+    rid, pid, se = topo.addr(c)
+    return bass.DstId(rid=rid, pnc=pid)
+
+
+def rank_program(g, core, T, topo):
+    chip = topo.chip(core)
+    ranks_of = lambda ch: [c for c in T.cores if topo.chip(c) == ch]
+    plane = [c for c in T.cores if (topo.chip(c) & 1) == (chip & 1)]
+    plane_chips = sorted({topo.chip(c) for c in plane})
+
+    if T.rank_of(core) is not None:
+        slot = plane.index(core)
+        g.dma_start(out=T.xs[:], in_=T.x[:]).then_inc(T.sem.local, 16)
+        g.wait_ge(T.sem.local, 16)
+        helpers = [ch * 8 + HELPER for ch in plane_chips]
+        g.remote_dma_fused(
+            [bass.RemoteDMATransfer(
+                dst_ids=[dst_id(topo, h) for h in helpers], dma_engine_mask=M_GATHER, remote_sem=T.sem.arr,
+                srcs=[T.xs[:]], dsts=[T.land[:, 2 * slot:2 * slot + 2] for h in helpers], alu_op=0)],
+            local_sem=T.sem.sent)
+        g.wait_ge(T.sem.got_a, bits(M_ON))
+        g.dma_start(out=T.y[:], in_=T.a[:]).then_inc(T.sem.local, 16)
+        g.wait_ge(T.sem.got_b, bits(M_MATE))
+        g.wait_ge(T.sem.local, 32)
+        g.dma_start(out=T.y[:], in_=T.b[:], accum_op=AluOpType.add).then_inc(T.sem.local, 16)
+        g.wait_ge(T.sem.sent, bits(M_GATHER))
+        g.wait_ge(T.sem.local, 48)
+        return
+
+    if core % 8 == HELPER and plane:
+        srcs = [T.land[:, 2 * i:2 * i + 2] for i in range(len(plane))]
+        here, mate = ranks_of(chip), ranks_of(chip ^ 1)
+        g.wait_ge(T.sem.arr, len(plane) * bits(M_GATHER))
+        g.remote_dma_fused(
+            [bass.RemoteDMATransfer(
+                dst_ids=[dst_id(topo, c) for c in here], dma_engine_mask=M_ON, remote_sem=T.sem.got_a,
+                srcs=srcs, dsts=[T.a[:] for c in here], alu_op=1),
+             bass.RemoteDMATransfer(
+                dst_ids=[dst_id(topo, c) for c in mate], dma_engine_mask=M_MATE, remote_sem=T.sem.got_b,
+                srcs=srcs, dsts=[T.b[:] for c in mate], alu_op=1)],
+            local_sem=T.sem.sent)
+        g.wait_ge(T.sem.sent, bits(M_ON) + bits(M_MATE))

@@ -1,7 +1,7 @@
 import concourse.bass as bass
 from concourse.mybir import AluOpType
 
-WHERE = "sbuf"
+WHERE = "dram"
 HELPER = 3
 M_GATHER = 0x00FF
 M_ON = 0xFF00
@@ -9,7 +9,7 @@ M_MATE = 0x00FF
 
 SCRATCH = {
     "xs": (WHERE, [128, 2], "float32"),
-    "land": (WHERE, [128, 12], "float32"),
+    "land": (WHERE, [6, 128, 2], "float32"),
     "a": (WHERE, [128, 2], "float32"),
     "b": (WHERE, [128, 2], "float32"),
 }
@@ -39,7 +39,7 @@ def rank_program(g, core, T, topo):
         g.remote_dma_fused(
             [bass.RemoteDMATransfer(
                 dst_ids=[dst_id(topo, h) for h in helpers], dma_engine_mask=M_GATHER, remote_sem=T.sem.arr,
-                srcs=[T.xs[:]], dsts=[T.land[:, 2 * slot:2 * slot + 2] for h in helpers], alu_op=0)],
+                srcs=[T.xs[:]], dsts=[T.land[slot] for h in helpers], alu_op=0)],
             local_sem=T.sem.sent)
         g.wait_ge(T.sem.got_a, bits(M_ON))
         g.dma_start(out=T.y[:], in_=T.a[:]).then_inc(T.sem.local, 16)
@@ -51,7 +51,7 @@ def rank_program(g, core, T, topo):
         return
 
     if core % 8 == HELPER and plane:
-        srcs = [T.land[:, 2 * i:2 * i + 2] for i in range(len(plane))]
+        srcs = [T.land[i] for i in range(len(plane))]
         here, mate = ranks_of(chip), ranks_of(chip ^ 1)
         g.wait_ge(T.sem.arr, len(plane) * bits(M_GATHER))
         g.remote_dma_fused(

@@ -1,23 +1,15 @@
 import concourse.bass as bass
-from concourse.mybir import AluOpType
 
-WHERE = "dram"
 HELPER = 3
-M_GATHER = 0x00FF
-M_ON = 0xFF00
-M_MATE = 0x00FF
+M_OFF = 0x00FF
+M_ON = 0xFFFF
 
 SCRATCH = {
-    "xs": (WHERE, [128, 2], "float32"),
-    "land": (WHERE, [6, 128, 2], "float32"),
-    "a": (WHERE, [128, 2], "float32"),
-    "b": (WHERE, [128, 2], "float32"),
+    "xs": ("dram", [128, 2], "float32"),
+    "land": ("dram", [7, 128, 2], "float32"),
+    "tot": ("dram", [128, 2], "float32"),
 }
-SEMAPHORES = ["local", "sent", "arr", "got_a", "got_b"]
-
-
-def bits(m):
-    return bin(m).count("1")
+SEMAPHORES = ["local", "sent", "arr", "arr_mate", "got"]
 
 
 def dst_id(topo, c):
@@ -27,39 +19,38 @@ def dst_id(topo, c):
 
 def rank_program(g, core, T, topo):
     chip = topo.chip(core)
-    ranks_of = lambda ch: [c for c in T.cores if topo.chip(c) == ch]
     plane = [c for c in T.cores if (topo.chip(c) & 1) == (chip & 1)]
-    plane_chips = sorted({topo.chip(c) for c in plane})
+    n = len(plane)
 
     if T.rank_of(core) is not None:
         slot = plane.index(core)
+        chips = sorted({topo.chip(c) for c in plane}, key=lambda ch: ch == chip)
+        helpers = [ch * 8 + HELPER for ch in chips]
         g.dma_start(out=T.xs[:], in_=T.x[:]).then_inc(T.sem.local, 16)
         g.wait_ge(T.sem.local, 16)
-        helpers = [ch * 8 + HELPER for ch in plane_chips]
         g.remote_dma_fused(
             [bass.RemoteDMATransfer(
-                dst_ids=[dst_id(topo, h) for h in helpers], dma_engine_mask=M_GATHER, remote_sem=T.sem.arr,
+                dst_ids=[dst_id(topo, h) for h in helpers], dma_engine_mask=M_OFF, remote_sem=T.sem.arr,
                 srcs=[T.xs[:]], dsts=[T.land[slot] for h in helpers], alu_op=0)],
             local_sem=T.sem.sent)
-        g.wait_ge(T.sem.got_a, bits(M_ON))
-        g.dma_start(out=T.y[:], in_=T.a[:]).then_inc(T.sem.local, 16)
-        g.wait_ge(T.sem.got_b, bits(M_MATE))
+        g.wait_ge(T.sem.got, 16)
+        g.dma_start(out=T.y[:], in_=T.tot[:]).then_inc(T.sem.local, 16)
+        g.wait_ge(T.sem.sent, 8)
         g.wait_ge(T.sem.local, 32)
-        g.dma_start(out=T.y[:], in_=T.b[:], accum_op=AluOpType.add).then_inc(T.sem.local, 16)
-        g.wait_ge(T.sem.sent, bits(M_GATHER))
-        g.wait_ge(T.sem.local, 48)
         return
 
     if core % 8 == HELPER and plane:
-        srcs = [T.land[i] for i in range(len(plane))]
-        here, mate = ranks_of(chip), ranks_of(chip ^ 1)
-        g.wait_ge(T.sem.arr, len(plane) * bits(M_GATHER))
+        here = [c for c in T.cores if topo.chip(c) == chip]
+        g.wait_ge(T.sem.arr, n * 8)
         g.remote_dma_fused(
             [bass.RemoteDMATransfer(
-                dst_ids=[dst_id(topo, c) for c in here], dma_engine_mask=M_ON, remote_sem=T.sem.got_a,
-                srcs=srcs, dsts=[T.a[:] for c in here], alu_op=1),
-             bass.RemoteDMATransfer(
-                dst_ids=[dst_id(topo, c) for c in mate], dma_engine_mask=M_MATE, remote_sem=T.sem.got_b,
-                srcs=srcs, dsts=[T.b[:] for c in mate], alu_op=1)],
+                dst_ids=[dst_id(topo, (chip ^ 1) * 8 + HELPER)], dma_engine_mask=M_OFF, remote_sem=T.sem.arr_mate,
+                srcs=[T.land[i] for i in range(n)], dsts=[T.land[n]], alu_op=1)],
             local_sem=T.sem.sent)
-        g.wait_ge(T.sem.sent, bits(M_ON) + bits(M_MATE))
+        g.wait_ge(T.sem.arr_mate, 8)
+        g.remote_dma_fused(
+            [bass.RemoteDMATransfer(
+                dst_ids=[dst_id(topo, c) for c in here], dma_engine_mask=M_ON, remote_sem=T.sem.got,
+                srcs=[T.land[i] for i in range(n + 1)], dsts=[T.tot[:] for c in here], alu_op=1)],
+            local_sem=T.sem.sent)
+        g.wait_ge(T.sem.sent, 8 + 16)

import concourse.bass as bass

HELPER = 3
M_OFF = 0x00FF
M_ON = 0xFFFF

SCRATCH = {
    "xs": ("dram", [128, 2], "float32"),
    "land": ("dram", [7, 128, 2], "float32"),
    "tot": ("dram", [128, 2], "float32"),
}
SEMAPHORES = ["local", "sent", "arr", "arr_mate", "got"]


def dst_id(topo, c):
    rid, pid, se = topo.addr(c)
    return bass.DstId(rid=rid, pnc=pid)


def rank_program(g, core, T, topo):
    chip = topo.chip(core)
    plane = [c for c in T.cores if (topo.chip(c) & 1) == (chip & 1)]
    n = len(plane)

    if T.rank_of(core) is not None:
        slot = plane.index(core)
        chips = sorted({topo.chip(c) for c in plane}, key=lambda ch: ch == chip)
        helpers = [ch * 8 + HELPER for ch in chips]
        g.dma_start(out=T.xs[:], in_=T.x[:]).then_inc(T.sem.local, 16)
        g.wait_ge(T.sem.local, 16)
        g.remote_dma_fused(
            [bass.RemoteDMATransfer(
                dst_ids=[dst_id(topo, h) for h in helpers], dma_engine_mask=M_OFF, remote_sem=T.sem.arr,
                srcs=[T.xs[:]], dsts=[T.land[slot] for h in helpers], alu_op=0)],
            local_sem=T.sem.sent)
        g.wait_ge(T.sem.got, 16)
        g.dma_start(out=T.y[:], in_=T.tot[:]).then_inc(T.sem.local, 16)
        g.wait_ge(T.sem.sent, 8)
        g.wait_ge(T.sem.local, 32)
        return

    if core % 8 == HELPER and plane:
        here = [c for c in T.cores if topo.chip(c) == chip]
        g.wait_ge(T.sem.arr, n * 8)
        g.remote_dma_fused(
            [bass.RemoteDMATransfer(
                dst_ids=[dst_id(topo, (chip ^ 1) * 8 + HELPER)], dma_engine_mask=M_OFF, remote_sem=T.sem.arr_mate,
                srcs=[T.land[i] for i in range(n)], dsts=[T.land[n]], alu_op=1)],
            local_sem=T.sem.sent)
        g.wait_ge(T.sem.arr_mate, 8)
        g.remote_dma_fused(
            [bass.RemoteDMATransfer(
                dst_ids=[dst_id(topo, c) for c in here], dma_engine_mask=M_ON, remote_sem=T.sem.got,
                srcs=[T.land[i] for i in range(n + 1)], dsts=[T.tot[:] for c in here], alu_op=1)],
            local_sem=T.sem.sent)
        g.wait_ge(T.sem.sent, 8 + 16)
